import numpy as np
import ml_dtypes


def mxq(x, axis, fmt="e4m3"):
    dtype, down = {"e4m3": (ml_dtypes.float8_e4m3fn, 7), "e5m2": (ml_dtypes.float8_e5m2, 14)}[fmt]
    v = np.moveaxis(np.asarray(x, np.float32).astype(ml_dtypes.bfloat16).astype(np.float64), axis, -1)
    blocks = v.reshape(v.shape[:-1] + (-1, 32))
    amax = np.abs(blocks).max(-1, keepdims=True)
    byte = np.maximum(np.where(amax > 0, np.frexp(amax)[1] - 1 + 127, 0) - down, 1)
    scale = np.exp2(byte - 127.0)
    codes = (blocks / scale).astype(np.float32).astype(dtype).astype(np.float64)
    return np.moveaxis((codes * scale).reshape(v.shape), -1, axis)


WIDE = False


def mx_kscale(k):
    if not WIDE:
        return np.ones(k)
    levels = np.array([10, -10, 5, -5, 0])
    if k % 512:
        return np.exp2(np.random.permutation(np.resize(levels, k // 32))).repeat(32)
    a = np.empty((k // 512, 16))
    for p in range(k // 512):
        a[p, :8] = np.random.permutation(np.resize(levels, 8))
        for g in range(8):
            far = levels[np.abs(levels - a[p, g]) >= 10]
            a[p, g + 8] = far[np.random.randint(len(far))]
    return np.exp2(a.ravel()).repeat(32)


def f64(x):
    return np.asarray(x).astype(np.float64)


def striped8(idx):
    return np.asarray(idx).reshape(8, -1, 16).transpose(0, 2, 1).reshape(128, -1).astype(np.uint16)


def unstriped8(offs):
    return offs.reshape(8, 16, -1).transpose(0, 2, 1).reshape(8, -1).astype(np.int64)


def pick8(x, idx, run):
    r = np.arange(len(x))
    return x[r[:, None], idx[r % (8 * run) // run]]


E2M1 = np.array([0.0, 0.5, 1.0, 1.5, 2.0, 3.0, 4.0, 6.0, -0.0, -0.5, -1.0, -1.5, -2.0, -3.0, -4.0, -6.0])


def pack_weight(w, fmt):
    k, n = w.shape
    w = f64(np.asarray(w, np.float32).astype(ml_dtypes.bfloat16)).reshape(k // 32, 32, n)
    amax = np.abs(w).max(1)
    if fmt == "e4m3":
        byte = np.frexp(amax)[1] - 1 + 127 - 7
    else:
        mant, ex = np.frexp(amax / 6.0)
        byte = np.where(mant > 0.5, ex, ex - 1) + 127
    byte = np.clip(np.where(amax > 0, byte, 1), 1, 254)
    scaled = (w * np.exp2(127.0 - byte)[:, None, :]).reshape(k, n).astype(np.float32)
    by_word = np.ascontiguousarray(scaled.reshape(k // 512, 128, 4, n).transpose(0, 1, 3, 2))
    if fmt == "e4m3":
        words = by_word.astype(ml_dtypes.float8_e4m3fn).view(np.uint8)
    else:
        c = by_word.astype(ml_dtypes.float4_e2m1fn).view(np.uint8) & 0xF
        words = (c[..., 0::2] | (c[..., 1::2] << 4)).reshape(k // 512, 128, 2 * n)
    return np.ascontiguousarray(words), np.ascontiguousarray(byte.astype(np.uint8).reshape(k // 512, 16, n))


def unpack_weight(words, scales, fmt):
    g, _, n = scales.shape
    words = np.ascontiguousarray(words).reshape(g, 128, n, -1)
    if fmt == "e4m3":
        vals = words.view(ml_dtypes.float8_e4m3fn).astype(np.float64)
    else:
        nib = np.empty((g, 128, n, 4), np.uint8)
        nib[..., 0::2] = words & 0xF
        nib[..., 1::2] = words >> 4
        vals = E2M1[nib]
    vals = vals * np.repeat(np.exp2(scales.astype(np.float64) - 127.0), 8, axis=1)[..., None]
    return vals.transpose(0, 1, 3, 2).reshape(g * 512, n)


D, T, I, Q = 512, 1024, 512, 128


def setup_inputs():
    n = np.random.standard_normal
    idx = np.stack([np.random.permutation(T)[:I] for _ in range(8)])
    idx2 = np.stack([np.random.permutation(T)[:I] for _ in range(8)])
    idx3 = np.stack([np.random.permutation(T)[:I] for _ in range(8)])
    fd = mx_kscale(D)
    keysp = pack_weight(n((D, T)) / fd[:, None], "e4m3")
    return {
        "query": (n((D, Q)) * 0.9 / np.sqrt(D) * fd[:, None]).astype(np.float32),
        "query2": (n((D, Q)) * 0.9 / np.sqrt(D) * fd[:, None]).astype(np.float32),
        "keys_words": keysp[0],
        "keys_scales": keysp[1],
        "lam": (np.random.uniform(0.5, 1.5, (Q, 1))).astype(np.float32),
        "old": (1.0 * n((Q, T))).astype(np.float32),
        "offs": striped8(idx),
        "offs2": striped8(idx2),
        "offs3": striped8(idx3),
    }


def reference(query, query2, keys_words, keys_scales, lam, old, offs, offs2, offs3):
    idx = unstriped8(offs)
    idx2 = unstriped8(offs2)
    idx3 = unstriped8(offs3)
    keysu = unpack_weight(keys_words, keys_scales, "e4m3")
    queryq = mxq(f64(query), 0, "e4m3")
    a = queryq.T @ keysu
    query2q = mxq(f64(query2), 0, "e4m3")
    b = query2q.T @ keysu
    w = pick8(a, idx, 16) + pick8(a, idx2, 16) * np.tanh(pick8(b, idx, 16)) * f64(lam)
    f1 = np.zeros((Q, T))
    f1[np.arange(Q)[:, None], idx[np.arange(Q) % 128 // 16]] = w
    f2 = f1 + f64(old)
    y = pick8(f2, idx3, 16)
    return y

@@ -1,0 +1,123 @@
+from contextlib import ExitStack
+
+import concourse.mybir as mybir
+
+D, T, I, Q = 512, 1024, 512, 128
+FLOPS = 2 * 2 * D * Q * T
+
+F32 = mybir.dt.float32
+BF16 = mybir.dt.bfloat16
+U32 = mybir.dt.uint32
+I32 = mybir.dt.int32
+U16 = mybir.dt.uint16
+U8 = mybir.dt.uint8
+FP8X4 = mybir.dt.float8_e4m3fn_x4
+ALU = mybir.AluOpType
+ACT = mybir.ActivationFunctionType
+
+P = 128
+PACK = 4
+PIECE = 256
+KEY_LOAD = 512
+HALF = I // 2
+LIST_COLS = I // 16
+
+
+def tile_attend_turnedby_lean_through_heads_kernel(tc, query, query2, keys_words, keys_scales, lam, old, offs, offs2, offs3, out):
+    nc = tc.nc
+    with ExitStack() as ctx:
+        keep = ctx.enter_context(tc.tile_pool(name="keep", bufs=1))
+        psum = ctx.enter_context(tc.psum_pool(name="psum", bufs=1))
+
+        key_scale = keep.tile([P, T], U8, align_bytes=64, name="key_scale")
+        nc.vector.memset(key_scale[:].bitcast(U32), 0)
+        f1 = keep.tile([P, T], F32, name="f1")
+        nc.vector.memset(f1[:], 0.0)
+
+        idx = keep.tile([P, LIST_COLS], U16, name="idx")
+        nc.sync.dma_start(idx[:], offs)
+        raw_b = keep.tile([P, PACK, Q], F32, name="raw_b")
+        nc.sync.dma_start(out=raw_b[:], in_=query2.rearrange("(p j) q -> p j q", j=PACK))
+        raw_a = keep.tile([P, PACK, Q], F32, name="raw_a")
+        nc.sync.dma_start(out=raw_a[:], in_=query.rearrange("(p j) q -> p j q", j=PACK))
+        for r in range(4):
+            nc.sync.dma_start(out=key_scale[r:P:32, :].bitcast(I32), in_=keys_scales[0][r:16:4, :].bitcast(I32))
+        words = keys_words[0].rearrange("p n t -> p (n t)")
+        key_words = []
+        for u in range(T // KEY_LOAD):
+            kw = keep.tile([P, KEY_LOAD], U32, align_bytes=64, name="key_words%d" % u)
+            nc.sync.dma_start(out=kw[:].bitcast(I32), in_=words[:, u * KEY_LOAD * PACK:(u + 1) * KEY_LOAD * PACK].bitcast(I32))
+            key_words.append(kw)
+        lam_sb = keep.tile([P, 1], F32, name="lam_sb")
+        nc.sync.dma_start(out=lam_sb[:], in_=lam)
+        idx2 = keep.tile([P, LIST_COLS], U16, name="idx2")
+        nc.sync.dma_start(idx2[:], offs2)
+        old_sb = keep.tile([P, T], F32, name="old_sb")
+        nc.sync.dma_start(out=old_sb[:], in_=old)
+        idx3 = keep.tile([P, LIST_COLS], U16, name="idx3")
+        nc.sync.dma_start(idx3[:], offs3)
+
+        two_lam = keep.tile([P, 1], F32, name="two_lam")
+        nc.gpsimd.tensor_scalar(two_lam[:], lam_sb[:], 2.0, 0.0, ALU.mult, ALU.add)
+        neg_lam = keep.tile([P, 1], F32, name="neg_lam")
+        nc.gpsimd.tensor_scalar(neg_lam[:], lam_sb[:], -1.0, 0.0, ALU.mult, ALU.add)
+
+        def quantise(raw, name):
+            grouped = keep.tile([P, Q, PACK], BF16, align_bytes=64, name=name + "_bf16", tag="grouped")
+            nc.vector.tensor_copy(out=grouped[:], in_=raw[:].rearrange("p j q -> p q j"))
+            codes = keep.tile([P, Q], U32, align_bytes=64, name=name + "_codes")
+            scales = keep.tile([P, Q], U8, align_bytes=64, name=name + "_scales")
+            nc.vector.quantize_mx(out=codes[:].bitcast(FP8X4), scales=scales[:], in_=grouped[:].rearrange("p q j -> p (q j)"))
+            return codes, scales
+
+        def score(codes, scales, name):
+            result = keep.tile([P, T], F32, name=name)
+            for c0 in range(0, T, PIECE):
+                bank = psum.tile([P, PIECE], F32, name="%s_bank%d" % (name, c0))
+                kw = key_words[c0 // KEY_LOAD]
+                k0 = c0 % KEY_LOAD
+                nc.tensor.matmul_mx(out=bank[:], lhsT=codes[:].bitcast(FP8X4), lhsT_scale=scales[:],
+                                    rhs=kw[:, k0:k0 + PIECE].bitcast(FP8X4), rhs_scale=key_scale[:, c0:c0 + PIECE],
+                                    start=True, stop=True)
+                nc.vector.tensor_copy(out=result[:, c0:c0 + PIECE], in_=bank[:])
+            return result
+
+        qb = quantise(raw_b, "qb")
+        qa = quantise(raw_a, "qa")
+        b = score(qb[0], qb[1], "b")
+        a = score(qa[0], qa[1], "a")
+
+        first = slice(0, LIST_COLS // 2)
+        second = slice(LIST_COLS // 2, LIST_COLS)
+
+        sig0 = keep.tile([P, HALF], F32, name="sig0")
+        nc.scalar.activation(sig0[:], b[:].indirect(idx[:, first]), ACT.Sigmoid, scale=2.0)
+        lean0 = keep.tile([P, HALF], F32, name="lean0", tag="turn")
+        nc.scalar.activation(lean0[:], sig0[:], ACT.Identity, bias=neg_lam[:], scale=two_lam[:])
+        own0 = keep.tile([P, HALF], F32, name="own0")
+        nc.scalar.activation(own0[:], a[:].indirect(idx[:, first]), ACT.Copy)
+        prod0 = keep.tile([P, HALF], F32, name="prod0")
+        nc.vector.tensor_tensor(prod0[:], a[:].indirect(idx2[:, first]), lean0[:], ALU.mult)
+        nc.vector.tensor_tensor(f1[:].indirect(idx[:, first]), own0[:], prod0[:], ALU.add)
+
+        sig1 = keep.tile([P, HALF], F32, name="sig1", tag="turn")
+        nc.scalar.activation(sig1[:], b[:].indirect(idx[:, second]), ACT.Sigmoid, scale=2.0)
+        lean1 = keep.tile([P, HALF], F32, name="lean1")
+        nc.scalar.activation(lean1[:], sig1[:], ACT.Identity, bias=neg_lam[:], scale=two_lam[:])
+        other1 = keep.tile([P, HALF], F32, name="other1")
+        nc.scalar.activation(other1[:], a[:].indirect(idx2[:, second]), ACT.Copy)
+        own1 = keep.tile([P, HALF], F32, name="own1", tag="turn")
+        nc.scalar.activation(own1[:], a[:].indirect(idx[:, second]), ACT.Copy)
+        prod1 = keep.tile([P, HALF], F32, name="prod1")
+        nc.vector.tensor_tensor(prod1[:], other1[:], lean1[:], ALU.mult)
+        nc.vector.tensor_tensor(f1[:].indirect(idx[:, second]), own1[:], prod1[:], ALU.add)
+
+        f2 = keep.tile([P, T], F32, name="f2")
+        nc.vector.tensor_tensor(f2[:], f1[:], old_sb[:], ALU.add)
+
+        y0 = keep.tile([P, HALF], F32, name="y0")
+        nc.vector.tensor_copy(y0[:], f2[:].indirect(idx3[:, first]))
+        nc.sync.dma_start(out=out[:, 0:HALF], in_=y0[:])
+        y1 = keep.tile([P, HALF], F32, name="y1")
+        nc.scalar.activation(y1[:], f2[:].indirect(idx3[:, second]), ACT.Copy)
+        nc.scalar.dma_start(out=out[:, HALF:I], in_=y1[:])

@@ -31,11 +31,12 @@ def tile_attend_turnedby_lean_through_heads_kernel(tc, query, query2, keys_words
 
         key_scale = keep.tile([P, T], U8, align_bytes=64, name="key_scale")
         nc.vector.memset(key_scale[:].bitcast(U32), 0)
+        warm = keep.tile([P, 2], F32, name="warm")
+        nc.gpsimd.memset(warm[:, 0:1], 0.0)
+        nc.scalar.activation(warm[:, 1:2], warm[:, 0:1], ACT.Sigmoid)
         f1 = keep.tile([P, T], F32, name="f1")
         nc.vector.memset(f1[:], 0.0)
 
-        idx = keep.tile([P, LIST_COLS], U16, name="idx")
-        nc.sync.dma_start(idx[:], offs)
         raw_b = keep.tile([P, PACK, Q], F32, name="raw_b")
         nc.sync.dma_start(out=raw_b[:], in_=query2.rearrange("(p j) q -> p j q", j=PACK))
         raw_a = keep.tile([P, PACK, Q], F32, name="raw_a")
@@ -48,6 +49,8 @@ def tile_attend_turnedby_lean_through_heads_kernel(tc, query, query2, keys_words
             kw = keep.tile([P, KEY_LOAD], U32, align_bytes=64, name="key_words%d" % u)
             nc.sync.dma_start(out=kw[:].bitcast(I32), in_=words[:, u * KEY_LOAD * PACK:(u + 1) * KEY_LOAD * PACK].bitcast(I32))
             key_words.append(kw)
+        idx = keep.tile([P, LIST_COLS], U16, name="idx")
+        nc.sync.dma_start(idx[:], offs)
         lam_sb = keep.tile([P, 1], F32, name="lam_sb")
         nc.sync.dma_start(out=lam_sb[:], in_=lam)
         idx2 = keep.tile([P, LIST_COLS], U16, name="idx2")
@@ -62,15 +65,18 @@ def tile_attend_turnedby_lean_through_heads_kernel(tc, query, query2, keys_words
         neg_lam = keep.tile([P, 1], F32, name="neg_lam")
         nc.gpsimd.tensor_scalar(neg_lam[:], lam_sb[:], -1.0, 0.0, ALU.mult, ALU.add)
 
-        def quantise(raw, name):
-            grouped = keep.tile([P, Q, PACK], BF16, align_bytes=64, name=name + "_bf16", tag="grouped")
-            nc.vector.tensor_copy(out=grouped[:], in_=raw[:].rearrange("p j q -> p q j"))
+        def quantise(raw, name, on_scalar):
+            grouped = keep.tile([P, Q, PACK], BF16, align_bytes=64, name=name + "_bf16")
+            if on_scalar:
+                nc.scalar.activation(grouped[:], raw[:].rearrange("p j q -> p q j"), ACT.Copy)
+            else:
+                nc.vector.tensor_copy(out=grouped[:], in_=raw[:].rearrange("p j q -> p q j"))
             codes = keep.tile([P, Q], U32, align_bytes=64, name=name + "_codes")
             scales = keep.tile([P, Q], U8, align_bytes=64, name=name + "_scales")
             nc.vector.quantize_mx(out=codes[:].bitcast(FP8X4), scales=scales[:], in_=grouped[:].rearrange("p q j -> p (q j)"))
             return codes, scales
 
-        def score(codes, scales, name):
+        def score(codes, scales, name, shared):
             result = keep.tile([P, T], F32, name=name)
             for c0 in range(0, T, PIECE):
                 bank = psum.tile([P, PIECE], F32, name="%s_bank%d" % (name, c0))
@@ -79,34 +85,37 @@ def tile_attend_turnedby_lean_through_heads_kernel(tc, query, query2, keys_words
                 nc.tensor.matmul_mx(out=bank[:], lhsT=codes[:].bitcast(FP8X4), lhsT_scale=scales[:],
                                     rhs=kw[:, k0:k0 + PIECE].bitcast(FP8X4), rhs_scale=key_scale[:, c0:c0 + PIECE],
                                     start=True, stop=True)
-                nc.vector.tensor_copy(out=result[:, c0:c0 + PIECE], in_=bank[:])
+                if shared and (c0 // PIECE) % 2 == 1:
+                    nc.scalar.activation(result[:, c0:c0 + PIECE], bank[:], ACT.Copy)
+                else:
+                    nc.vector.tensor_copy(out=result[:, c0:c0 + PIECE], in_=bank[:])
             return result
 
-        qb = quantise(raw_b, "qb")
-        qa = quantise(raw_a, "qa")
-        b = score(qb[0], qb[1], "b")
-        a = score(qa[0], qa[1], "a")
+        qb = quantise(raw_b, "qb", False)
+        qa = quantise(raw_a, "qa", True)
+        b = score(qb[0], qb[1], "b", True)
+        a = score(qa[0], qa[1], "a", False)
 
         first = slice(0, LIST_COLS // 2)
         second = slice(LIST_COLS // 2, LIST_COLS)
 
         sig0 = keep.tile([P, HALF], F32, name="sig0")
         nc.scalar.activation(sig0[:], b[:].indirect(idx[:, first]), ACT.Sigmoid, scale=2.0)
-        lean0 = keep.tile([P, HALF], F32, name="lean0", tag="turn")
-        nc.scalar.activation(lean0[:], sig0[:], ACT.Identity, bias=neg_lam[:], scale=two_lam[:])
+        sig1 = keep.tile([P, HALF], F32, name="sig1")
+        nc.scalar.activation(sig1[:], b[:].indirect(idx[:, second]), ACT.Sigmoid, scale=2.0)
+        lean0 = keep.tile([P, HALF], F32, name="lean0", tag="lean")
+        nc.vector.tensor_scalar(lean0[:], sig0[:], two_lam[:], neg_lam[:], ALU.mult, ALU.add)
         own0 = keep.tile([P, HALF], F32, name="own0")
         nc.scalar.activation(own0[:], a[:].indirect(idx[:, first]), ACT.Copy)
         prod0 = keep.tile([P, HALF], F32, name="prod0")
         nc.vector.tensor_tensor(prod0[:], a[:].indirect(idx2[:, first]), lean0[:], ALU.mult)
         nc.vector.tensor_tensor(f1[:].indirect(idx[:, first]), own0[:], prod0[:], ALU.add)
 
-        sig1 = keep.tile([P, HALF], F32, name="sig1", tag="turn")
-        nc.scalar.activation(sig1[:], b[:].indirect(idx[:, second]), ACT.Sigmoid, scale=2.0)
-        lean1 = keep.tile([P, HALF], F32, name="lean1")
-        nc.scalar.activation(lean1[:], sig1[:], ACT.Identity, bias=neg_lam[:], scale=two_lam[:])
         other1 = keep.tile([P, HALF], F32, name="other1")
         nc.scalar.activation(other1[:], a[:].indirect(idx2[:, second]), ACT.Copy)
-        own1 = keep.tile([P, HALF], F32, name="own1", tag="turn")
+        lean1 = keep.tile([P, HALF], F32, name="lean1", tag="lean")
+        nc.scalar.activation(lean1[:], sig1[:], ACT.Identity, bias=neg_lam[:], scale=two_lam[:])
+        own1 = keep.tile([P, HALF], F32, name="own1")
         nc.scalar.activation(own1[:], a[:].indirect(idx[:, second]), ACT.Copy)
         prod1 = keep.tile([P, HALF], F32, name="prod1")
         nc.vector.tensor_tensor(prod1[:], other1[:], lean1[:], ALU.mult)

@@ -29,7 +29,7 @@ def tile_attend_turnedby_lean_through_heads_kernel(tc, query, query2, keys_words
         keep = ctx.enter_context(tc.tile_pool(name="keep", bufs=1))
         psum = ctx.enter_context(tc.psum_pool(name="psum", bufs=1))
 
-        key_scale = keep.tile([P, T], U8, align_bytes=64, name="key_scale")
+        key_scale = keep.tile([P, PIECE], U8, align_bytes=64, name="key_scale")
         nc.vector.memset(key_scale[:].bitcast(U32), 0)
         warm = keep.tile([P, 2], F32, name="warm")
         nc.gpsimd.memset(warm[:, 0:1], 0.0)
@@ -41,8 +41,9 @@ def tile_attend_turnedby_lean_through_heads_kernel(tc, query, query2, keys_words
         nc.sync.dma_start(out=raw_b[:], in_=query2.rearrange("(p j) q -> p j q", j=PACK))
         raw_a = keep.tile([P, PACK, Q], F32, name="raw_a")
         nc.sync.dma_start(out=raw_a[:], in_=query.rearrange("(p j) q -> p j q", j=PACK))
-        for r in range(4):
-            nc.sync.dma_start(out=key_scale[r:P:32, :].bitcast(I32), in_=keys_scales[0][r:16:4, :].bitcast(I32))
+        scale_rows = keys_scales[0].bitcast(I32).rearrange("f (h c) -> h f c", h=T // PIECE)
+        for quad in range(4):
+            nc.sync.dma_start(out=key_scale[32 * quad:32 * quad + 16, :].bitcast(I32), in_=scale_rows[:, 4 * quad:4 * quad + 4, :])
         words = keys_words[0].rearrange("p n t -> p (n t)")
         key_words = []
         for u in range(T // KEY_LOAD):
@@ -70,10 +71,14 @@ def tile_attend_turnedby_lean_through_heads_kernel(tc, query, query2, keys_words
             if on_scalar:
                 nc.scalar.activation(grouped[:], raw[:].rearrange("p j q -> p q j"), ACT.Copy)
             else:
-                nc.vector.tensor_copy(out=grouped[:], in_=raw[:].rearrange("p j q -> p q j"))
+                for h in range(2):
+                    nc.vector.tensor_copy(out=grouped[:, h * 64:(h + 1) * 64, :], in_=raw[:, :, h * 64:(h + 1) * 64].rearrange("p j q -> p q j"))
             codes = keep.tile([P, Q], U32, align_bytes=64, name=name + "_codes")
             scales = keep.tile([P, Q], U8, align_bytes=64, name=name + "_scales")
-            nc.vector.quantize_mx(out=codes[:].bitcast(FP8X4), scales=scales[:], in_=grouped[:].rearrange("p q j -> p (q j)"))
+            width = Q if on_scalar else Q // 2
+            for q0 in range(0, Q, width):
+                nc.vector.quantize_mx(out=codes[:, q0:q0 + width].bitcast(FP8X4), scales=scales[:, q0:q0 + width],
+                                      in_=grouped[:, q0:q0 + width, :].rearrange("p q j -> p (q j)"))
             return codes, scales
 
         def score(codes, scales, name, shared):
@@ -83,7 +88,7 @@ def tile_attend_turnedby_lean_through_heads_kernel(tc, query, query2, keys_words
                 kw = key_words[c0 // KEY_LOAD]
                 k0 = c0 % KEY_LOAD
                 nc.tensor.matmul_mx(out=bank[:], lhsT=codes[:].bitcast(FP8X4), lhsT_scale=scales[:],
-                                    rhs=kw[:, k0:k0 + PIECE].bitcast(FP8X4), rhs_scale=key_scale[:, c0:c0 + PIECE],
+                                    rhs=kw[:, k0:k0 + PIECE].bitcast(FP8X4), rhs_scale=key_scale[4 * (c0 // PIECE):P, :],
                                     start=True, stop=True)
                 if shared and (c0 // PIECE) % 2 == 1:
                     nc.scalar.activation(result[:, c0:c0 + PIECE], bank[:], ACT.Copy)

@@ -17,10 +17,16 @@ ACT = mybir.ActivationFunctionType
 
 P = 128
 PACK = 4
+QUADRANT = 32
+SCALE_ROWS = 4
+BANKS = 8
 PIECE = 256
 KEY_LOAD = 512
 HALF = I // 2
 LIST_COLS = I // 16
+
+B_PASSES = ((0, 256, False), (256, 512, True), (512, 768, False), (768, 896, True), (896, 1024, True))
+A_PASSES = tuple((c, c + PIECE, False) for c in range(0, T, PIECE))
 
 
 def tile_attend_turnedby_lean_through_heads_kernel(tc, query, query2, keys_words, keys_scales, lam, old, offs, offs2, offs3, out):
@@ -31,9 +37,11 @@ def tile_attend_turnedby_lean_through_heads_kernel(tc, query, query2, keys_words
 
         key_scale = keep.tile([P, PIECE], U8, align_bytes=64, name="key_scale")
         nc.vector.memset(key_scale[:].bitcast(U32), 0)
+
         warm = keep.tile([P, 2], F32, name="warm")
         nc.gpsimd.memset(warm[:, 0:1], 0.0)
         nc.scalar.activation(warm[:, 1:2], warm[:, 0:1], ACT.Sigmoid)
+
         f1 = keep.tile([P, T], F32, name="f1")
         nc.vector.memset(f1[:], 0.0)
 
@@ -42,14 +50,17 @@ def tile_attend_turnedby_lean_through_heads_kernel(tc, query, query2, keys_words
         raw_a = keep.tile([P, PACK, Q], F32, name="raw_a")
         nc.sync.dma_start(out=raw_a[:], in_=query.rearrange("(p j) q -> p j q", j=PACK))
         scale_rows = keys_scales[0].bitcast(I32).rearrange("f (h c) -> h f c", h=T // PIECE)
-        for quad in range(4):
-            nc.sync.dma_start(out=key_scale[32 * quad:32 * quad + 16, :].bitcast(I32), in_=scale_rows[:, 4 * quad:4 * quad + 4, :])
+        for quad in range(P // QUADRANT):
+            rows = slice(QUADRANT * quad, QUADRANT * quad + SCALE_ROWS * (T // PIECE))
+            nc.sync.dma_start(out=key_scale[rows, :].bitcast(I32),
+                              in_=scale_rows[:, SCALE_ROWS * quad:SCALE_ROWS * (quad + 1), :])
         words = keys_words[0].rearrange("p n t -> p (n t)")
         key_words = []
         for u in range(T // KEY_LOAD):
-            kw = keep.tile([P, KEY_LOAD], U32, align_bytes=64, name="key_words%d" % u)
-            nc.sync.dma_start(out=kw[:].bitcast(I32), in_=words[:, u * KEY_LOAD * PACK:(u + 1) * KEY_LOAD * PACK].bitcast(I32))
-            key_words.append(kw)
+            loaded = keep.tile([P, KEY_LOAD], U32, align_bytes=64, name="key_words%d" % u)
+            nc.sync.dma_start(out=loaded[:].bitcast(I32),
+                              in_=words[:, u * KEY_LOAD * PACK:(u + 1) * KEY_LOAD * PACK].bitcast(I32))
+            key_words.append(loaded)
         idx = keep.tile([P, LIST_COLS], U16, name="idx")
         nc.sync.dma_start(idx[:], offs)
         lam_sb = keep.tile([P, 1], F32, name="lam_sb")
@@ -66,40 +77,42 @@ def tile_attend_turnedby_lean_through_heads_kernel(tc, query, query2, keys_words
         neg_lam = keep.tile([P, 1], F32, name="neg_lam")
         nc.gpsimd.tensor_scalar(neg_lam[:], lam_sb[:], -1.0, 0.0, ALU.mult, ALU.add)
 
-        def quantise(raw, name, on_scalar):
-            grouped = keep.tile([P, Q, PACK], BF16, align_bytes=64, name=name + "_bf16")
-            if on_scalar:
-                nc.scalar.activation(grouped[:], raw[:].rearrange("p j q -> p q j"), ACT.Copy)
-            else:
-                for h in range(2):
-                    nc.vector.tensor_copy(out=grouped[:, h * 64:(h + 1) * 64, :], in_=raw[:, :, h * 64:(h + 1) * 64].rearrange("p j q -> p q j"))
+        def quantise(grouped, name, width):
             codes = keep.tile([P, Q], U32, align_bytes=64, name=name + "_codes")
             scales = keep.tile([P, Q], U8, align_bytes=64, name=name + "_scales")
-            width = Q if on_scalar else Q // 2
             for q0 in range(0, Q, width):
                 nc.vector.quantize_mx(out=codes[:, q0:q0 + width].bitcast(FP8X4), scales=scales[:, q0:q0 + width],
                                       in_=grouped[:, q0:q0 + width, :].rearrange("p q j -> p (q j)"))
             return codes, scales
 
-        def score(codes, scales, name, shared):
+        def score(quantised, name, passes, first_bank):
+            codes, scales = quantised
             result = keep.tile([P, T], F32, name=name)
-            for c0 in range(0, T, PIECE):
-                bank = psum.tile([P, PIECE], F32, name="%s_bank%d" % (name, c0))
-                kw = key_words[c0 // KEY_LOAD]
-                k0 = c0 % KEY_LOAD
+            for n, (c0, c1, on_scalar) in enumerate(passes):
+                bank = psum.tile([P, c1 - c0], F32, name="%s_bank%d" % (name, c0), tag="bank%d" % ((first_bank + n) % BANKS))
+                in_load = slice(c0 % KEY_LOAD, c0 % KEY_LOAD + c1 - c0)
+                in_piece = slice(c0 % PIECE, c0 % PIECE + c1 - c0)
                 nc.tensor.matmul_mx(out=bank[:], lhsT=codes[:].bitcast(FP8X4), lhsT_scale=scales[:],
-                                    rhs=kw[:, k0:k0 + PIECE].bitcast(FP8X4), rhs_scale=key_scale[4 * (c0 // PIECE):P, :],
+                                    rhs=key_words[c0 // KEY_LOAD][:, in_load].bitcast(FP8X4),
+                                    rhs_scale=key_scale[SCALE_ROWS * (c0 // PIECE):P, in_piece],
                                     start=True, stop=True)
-                if shared and (c0 // PIECE) % 2 == 1:
-                    nc.scalar.activation(result[:, c0:c0 + PIECE], bank[:], ACT.Copy)
+                if on_scalar:
+                    nc.scalar.activation(result[:, c0:c1], bank[:], ACT.Copy)
                 else:
-                    nc.vector.tensor_copy(out=result[:, c0:c0 + PIECE], in_=bank[:])
+                    nc.vector.tensor_copy(out=result[:, c0:c1], in_=bank[:])
             return result
 
-        qb = quantise(raw_b, "qb", False)
-        qa = quantise(raw_a, "qa", True)
-        b = score(qb[0], qb[1], "b", True)
-        a = score(qa[0], qa[1], "a", False)
+        grouped_b = keep.tile([P, Q, PACK], BF16, align_bytes=64, name="qb_bf16")
+        for q0 in range(0, Q, Q // 2):
+            cols = slice(q0, q0 + Q // 2)
+            nc.vector.tensor_copy(out=grouped_b[:, cols, :], in_=raw_b[:, :, cols].rearrange("p j q -> p q j"))
+        quantised_b = quantise(grouped_b, "qb", Q // 2)
+        grouped_a = keep.tile([P, Q, PACK], BF16, align_bytes=64, name="qa_bf16")
+        nc.scalar.activation(grouped_a[:], raw_a[:].rearrange("p j q -> p q j"), ACT.Copy)
+        quantised_a = quantise(grouped_a, "qa", Q)
+
+        b = score(quantised_b, "b", B_PASSES, 0)
+        a = score(quantised_a, "a", A_PASSES, len(B_PASSES))
 
         first = slice(0, LIST_COLS // 2)
         second = slice(LIST_COLS // 2, LIST_COLS)
@@ -108,6 +121,7 @@ def tile_attend_turnedby_lean_through_heads_kernel(tc, query, query2, keys_words
         nc.scalar.activation(sig0[:], b[:].indirect(idx[:, first]), ACT.Sigmoid, scale=2.0)
         sig1 = keep.tile([P, HALF], F32, name="sig1")
         nc.scalar.activation(sig1[:], b[:].indirect(idx[:, second]), ACT.Sigmoid, scale=2.0)
+
         lean0 = keep.tile([P, HALF], F32, name="lean0", tag="lean")
         nc.vector.tensor_scalar(lean0[:], sig0[:], two_lam[:], neg_lam[:], ALU.mult, ALU.add)
         own0 = keep.tile([P, HALF], F32, name="own0")

from contextlib import ExitStack

import concourse.mybir as mybir

D, T, I, Q = 512, 1024, 512, 128
FLOPS = 2 * 2 * D * Q * T

F32 = mybir.dt.float32
BF16 = mybir.dt.bfloat16
U32 = mybir.dt.uint32
I32 = mybir.dt.int32
U16 = mybir.dt.uint16
U8 = mybir.dt.uint8
FP8X4 = mybir.dt.float8_e4m3fn_x4
ALU = mybir.AluOpType
ACT = mybir.ActivationFunctionType

P = 128
PACK = 4
QUADRANT = 32
SCALE_ROWS = 4
BANKS = 8
PIECE = 256
KEY_LOAD = 512
HALF = I // 2
LIST_COLS = I // 16

B_PASSES = ((0, 256, False), (256, 512, True), (512, 768, False), (768, 896, True), (896, 1024, True))
A_PASSES = tuple((c, c + PIECE, False) for c in range(0, T, PIECE))


def tile_attend_turnedby_lean_through_heads_kernel(tc, query, query2, keys_words, keys_scales, lam, old, offs, offs2, offs3, out):
    nc = tc.nc
    with ExitStack() as ctx:
        keep = ctx.enter_context(tc.tile_pool(name="keep", bufs=1))
        psum = ctx.enter_context(tc.psum_pool(name="psum", bufs=1))

        key_scale = keep.tile([P, PIECE], U8, align_bytes=64, name="key_scale")
        nc.vector.memset(key_scale[:].bitcast(U32), 0)

        warm = keep.tile([P, 2], F32, name="warm")
        nc.gpsimd.memset(warm[:, 0:1], 0.0)
        nc.scalar.activation(warm[:, 1:2], warm[:, 0:1], ACT.Sigmoid)

        f1 = keep.tile([P, T], F32, name="f1")
        nc.vector.memset(f1[:], 0.0)

        raw_b = keep.tile([P, PACK, Q], F32, name="raw_b")
        nc.sync.dma_start(out=raw_b[:], in_=query2.rearrange("(p j) q -> p j q", j=PACK))
        raw_a = keep.tile([P, PACK, Q], F32, name="raw_a")
        nc.sync.dma_start(out=raw_a[:], in_=query.rearrange("(p j) q -> p j q", j=PACK))
        scale_rows = keys_scales[0].bitcast(I32).rearrange("f (h c) -> h f c", h=T // PIECE)
        for quad in range(P // QUADRANT):
            rows = slice(QUADRANT * quad, QUADRANT * quad + SCALE_ROWS * (T // PIECE))
            nc.sync.dma_start(out=key_scale[rows, :].bitcast(I32),
                              in_=scale_rows[:, SCALE_ROWS * quad:SCALE_ROWS * (quad + 1), :])
        words = keys_words[0].rearrange("p n t -> p (n t)")
        key_words = []
        for u in range(T // KEY_LOAD):
            loaded = keep.tile([P, KEY_LOAD], U32, align_bytes=64, name="key_words%d" % u)
            nc.sync.dma_start(out=loaded[:].bitcast(I32),
                              in_=words[:, u * KEY_LOAD * PACK:(u + 1) * KEY_LOAD * PACK].bitcast(I32))
            key_words.append(loaded)
        idx = keep.tile([P, LIST_COLS], U16, name="idx")
        nc.sync.dma_start(idx[:], offs)
        lam_sb = keep.tile([P, 1], F32, name="lam_sb")
        nc.sync.dma_start(out=lam_sb[:], in_=lam)
        idx2 = keep.tile([P, LIST_COLS], U16, name="idx2")
        nc.sync.dma_start(idx2[:], offs2)
        old_sb = keep.tile([P, T], F32, name="old_sb")
        nc.sync.dma_start(out=old_sb[:], in_=old)
        idx3 = keep.tile([P, LIST_COLS], U16, name="idx3")
        nc.sync.dma_start(idx3[:], offs3)

        two_lam = keep.tile([P, 1], F32, name="two_lam")
        nc.gpsimd.tensor_scalar(two_lam[:], lam_sb[:], 2.0, 0.0, ALU.mult, ALU.add)
        neg_lam = keep.tile([P, 1], F32, name="neg_lam")
        nc.gpsimd.tensor_scalar(neg_lam[:], lam_sb[:], -1.0, 0.0, ALU.mult, ALU.add)

        def quantise(grouped, name, width):
            codes = keep.tile([P, Q], U32, align_bytes=64, name=name + "_codes")
            scales = keep.tile([P, Q], U8, align_bytes=64, name=name + "_scales")
            for q0 in range(0, Q, width):
                nc.vector.quantize_mx(out=codes[:, q0:q0 + width].bitcast(FP8X4), scales=scales[:, q0:q0 + width],
                                      in_=grouped[:, q0:q0 + width, :].rearrange("p q j -> p (q j)"))
            return codes, scales

        def score(quantised, name, passes, first_bank):
            codes, scales = quantised
            result = keep.tile([P, T], F32, name=name)
            for n, (c0, c1, on_scalar) in enumerate(passes):
                bank = psum.tile([P, c1 - c0], F32, name="%s_bank%d" % (name, c0), tag="bank%d" % ((first_bank + n) % BANKS))
                in_load = slice(c0 % KEY_LOAD, c0 % KEY_LOAD + c1 - c0)
                in_piece = slice(c0 % PIECE, c0 % PIECE + c1 - c0)
                nc.tensor.matmul_mx(out=bank[:], lhsT=codes[:].bitcast(FP8X4), lhsT_scale=scales[:],
                                    rhs=key_words[c0 // KEY_LOAD][:, in_load].bitcast(FP8X4),
                                    rhs_scale=key_scale[SCALE_ROWS * (c0 // PIECE):P, in_piece],
                                    start=True, stop=True)
                if on_scalar:
                    nc.scalar.activation(result[:, c0:c1], bank[:], ACT.Copy)
                else:
                    nc.vector.tensor_copy(out=result[:, c0:c1], in_=bank[:])
            return result

        grouped_b = keep.tile([P, Q, PACK], BF16, align_bytes=64, name="qb_bf16")
        for q0 in range(0, Q, Q // 2):
            cols = slice(q0, q0 + Q // 2)
            nc.vector.tensor_copy(out=grouped_b[:, cols, :], in_=raw_b[:, :, cols].rearrange("p j q -> p q j"))
        quantised_b = quantise(grouped_b, "qb", Q // 2)
        grouped_a = keep.tile([P, Q, PACK], BF16, align_bytes=64, name="qa_bf16")
        nc.scalar.activation(grouped_a[:], raw_a[:].rearrange("p j q -> p q j"), ACT.Copy)
        quantised_a = quantise(grouped_a, "qa", Q)

        b = score(quantised_b, "b", B_PASSES, 0)
        a = score(quantised_a, "a", A_PASSES, len(B_PASSES))

        first = slice(0, LIST_COLS // 2)
        second = slice(LIST_COLS // 2, LIST_COLS)

        sig0 = keep.tile([P, HALF], F32, name="sig0")
        nc.scalar.activation(sig0[:], b[:].indirect(idx[:, first]), ACT.Sigmoid, scale=2.0)
        sig1 = keep.tile([P, HALF], F32, name="sig1")
        nc.scalar.activation(sig1[:], b[:].indirect(idx[:, second]), ACT.Sigmoid, scale=2.0)

        lean0 = keep.tile([P, HALF], F32, name="lean0", tag="lean")
        nc.vector.tensor_scalar(lean0[:], sig0[:], two_lam[:], neg_lam[:], ALU.mult, ALU.add)
        own0 = keep.tile([P, HALF], F32, name="own0")
        nc.scalar.activation(own0[:], a[:].indirect(idx[:, first]), ACT.Copy)
        prod0 = keep.tile([P, HALF], F32, name="prod0")
        nc.vector.tensor_tensor(prod0[:], a[:].indirect(idx2[:, first]), lean0[:], ALU.mult)
        nc.vector.tensor_tensor(f1[:].indirect(idx[:, first]), own0[:], prod0[:], ALU.add)

        other1 = keep.tile([P, HALF], F32, name="other1")
        nc.scalar.activation(other1[:], a[:].indirect(idx2[:, second]), ACT.Copy)
        lean1 = keep.tile([P, HALF], F32, name="lean1", tag="lean")
        nc.scalar.activation(lean1[:], sig1[:], ACT.Identity, bias=neg_lam[:], scale=two_lam[:])
        own1 = keep.tile([P, HALF], F32, name="own1")
        nc.scalar.activation(own1[:], a[:].indirect(idx[:, second]), ACT.Copy)
        prod1 = keep.tile([P, HALF], F32, name="prod1")
        nc.vector.tensor_tensor(prod1[:], other1[:], lean1[:], ALU.mult)
        nc.vector.tensor_tensor(f1[:].indirect(idx[:, second]), own1[:], prod1[:], ALU.add)

        f2 = keep.tile([P, T], F32, name="f2")
        nc.vector.tensor_tensor(f2[:], f1[:], old_sb[:], ALU.add)

        y0 = keep.tile([P, HALF], F32, name="y0")
        nc.vector.tensor_copy(y0[:], f2[:].indirect(idx3[:, first]))
        nc.sync.dma_start(out=out[:, 0:HALF], in_=y0[:])
        y1 = keep.tile([P, HALF], F32, name="y1")
        nc.scalar.activation(y1[:], f2[:].indirect(idx3[:, second]), ACT.Copy)
        nc.scalar.dma_start(out=out[:, HALF:I], in_=y1[:])
